import numpy as np
import ml_dtypes


def mxq(x, axis, fmt="e4m3"):
    dtype, down = {"e4m3": (ml_dtypes.float8_e4m3fn, 7), "e5m2": (ml_dtypes.float8_e5m2, 14)}[fmt]
    v = np.moveaxis(np.asarray(x, np.float32).astype(ml_dtypes.bfloat16).astype(np.float64), axis, -1)
    blocks = v.reshape(v.shape[:-1] + (-1, 32))
    amax = np.abs(blocks).max(-1, keepdims=True)
    byte = np.maximum(np.where(amax > 0, np.frexp(amax)[1] - 1 + 127, 0) - down, 1)
    scale = np.exp2(byte - 127.0)
    codes = (blocks / scale).astype(np.float32).astype(dtype).astype(np.float64)
    return np.moveaxis((codes * scale).reshape(v.shape), -1, axis)


WIDE = False


def mx_kscale(k):
    if not WIDE:
        return np.ones(k)
    levels = np.array([10, -10, 5, -5, 0])
    if k % 512:
        return np.exp2(np.random.permutation(np.resize(levels, k // 32))).repeat(32)
    a = np.empty((k // 512, 16))
    for p in range(k // 512):
        a[p, :8] = np.random.permutation(np.resize(levels, 8))
        for g in range(8):
            far = levels[np.abs(levels - a[p, g]) >= 10]
            a[p, g + 8] = far[np.random.randint(len(far))]
    return np.exp2(a.ravel()).repeat(32)


def f64(x):
    return np.asarray(x).astype(np.float64)


def striped(idx):
    return np.tile(idx.reshape(-1, 16).T, (8, 1)).astype(np.uint16)


def unstriped(offs):
    return offs[:16].T.reshape(-1).astype(np.int64)


def striped8(idx):
    return np.concatenate([x.reshape(-1, 16).T for x in idx]).astype(np.uint16)


def runs(offs, k):
    lists = np.stack([offs[16 * r : 16 * r + 16].T.reshape(-1) for r in range(8)]).astype(np.int64)
    return lists[np.arange(k) % 512 // 64]


def pack_weight(w):
    k, n = w.shape
    w = f64(np.asarray(w, np.float32).astype(ml_dtypes.bfloat16)).reshape(k // 32, 32, n)
    amax = np.abs(w).max(1)
    byte = np.clip(np.where(amax > 0, np.frexp(amax)[1] - 1 + 127 - 7, 1), 1, 254)
    scaled = (w * np.exp2(127.0 - byte)[:, None, :]).reshape(k, n).astype(np.float32)
    words = np.ascontiguousarray(scaled.reshape(k // 512, 128, 4, n).transpose(0, 1, 3, 2)).astype(ml_dtypes.float8_e4m3fn).view(np.uint8)
    return words, np.ascontiguousarray(byte.astype(np.uint8).reshape(k // 512, 16, n))


def unpack_weight(words, scales):
    g, p, n, _ = words.shape
    vals = np.ascontiguousarray(words).view(ml_dtypes.float8_e4m3fn).astype(np.float64) * np.repeat(np.exp2(scales.astype(np.float64) - 127.0), 8, axis=1)[..., None]
    return vals.transpose(0, 1, 3, 2).reshape(g * 512, n)


K, T, S, N, H = 512, 2048, 512, 512, 512


def setup_inputs():
    n = np.random.standard_normal
    s = mx_kscale(K)[:, None]
    u = mx_kscale(H)
    packed_xT = pack_weight(n((K, T)) * s)
    return {
        "x_words": packed_xT[0],
        "x_scales": packed_xT[1],
        "w1": (n((K, H)) / np.sqrt(K) / s).astype(np.float32),
        "gn": (np.random.uniform(0.5, 1.5, (H, 1)) * u[:, None]).astype(np.float32),
        "w2": (n((H, N)) / np.sqrt(H) / u[:, None]).astype(np.float32),
        "tau": np.random.uniform(0.5, 1.2, (N, 1)).astype(np.float32),
        "offs": striped8(np.random.randint(0, T, (8, S))),
        "n1": striped(np.random.permutation(S)),
        "n2": striped(np.random.permutation(S)),
        "n3": striped(np.random.permutation(S)),
        "n4": striped(np.random.permutation(S)),
        "n5": striped(np.random.permutation(S)),
    }


def reference(x_words, x_scales, w1, gn, w2, tau, offs, n1, n2, n3, n4, n5):
    xq = unpack_weight(x_words, x_scales)[np.arange(K)[:, None], runs(offs, K)]
    y = mxq(f64(w1), 0, "e4m3").T @ xq
    z = f64(gn) * (np.maximum(y, y[:, unstriped(n1)]) - (np.maximum(y[:, unstriped(n2)], y[:, unstriped(n3)])))
    h = mxq(f64(w2), 0, "e4m3").T @ mxq(z, 0, "e4m3")
    sz = np.abs(h)
    ea = np.exp(-1.0 * (f64(tau) * sz[:, unstriped(n4)]))
    return (h - h[:, unstriped(n5)]) * ea

@@ -1,0 +1,267 @@
+from contextlib import ExitStack
+
+import concourse.mybir as mybir
+
+K, T, S, N, H = 512, 2048, 512, 512, 512
+FLOPS = 2 * K * H * S + 2 * H * N * S
+
+F32 = mybir.dt.float32
+BF16 = mybir.dt.bfloat16
+I32 = mybir.dt.int32
+U32 = mybir.dt.uint32
+U16 = mybir.dt.uint16
+U8 = mybir.dt.uint8
+FP8X4 = mybir.dt.float8_e4m3fn_x4
+ALU = mybir.AluOpType
+ACT = mybir.ActivationFunctionType
+
+P = 128
+PACK = 4
+HALF = S // 2
+HALF_COLS = HALF // 16
+SCALAR_W1 = 80
+
+
+def tile_picked_hashmixela_none_p_kernel(
+    tc, x_words, x_scales, w1, gn, w2, tau, offs, n1, n2, n3, n4, n5, out
+):
+    nc = tc.nc
+    with ExitStack() as ctx:
+        keep = ctx.enter_context(tc.tile_pool(name="keep", bufs=1))
+        psum = ctx.enter_context(tc.psum_pool(name="psum", bufs=1))
+
+        def sbuf(name, cols, dtype, tag=""):
+            return keep.tile([P, cols], dtype, name=name, tag=tag or name, align_bytes=64)
+
+        def bank(name, number):
+            return psum.tile([P, 512], F32, name=name, tag="bank%d" % number)
+
+        def load_list(name, source):
+            tile = sbuf(name, S // 16, U16)
+            nc.sync.dma_start(tile[:], source)
+            return tile
+
+        def half(c):
+            return slice(c * HALF, (c + 1) * HALF)
+
+        def list_half(tile, c):
+            return tile[:, c * HALF_COLS : (c + 1) * HALF_COLS]
+
+        def gather(engine, dst, window, offsets):
+            if engine == "vector":
+                nc.vector.tensor_copy(dst, window[:].indirect(offsets))
+            else:
+                nc.scalar.activation(dst, window[:].indirect(offsets), ACT.Copy)
+
+        def plain_copy(engine, dst, source):
+            if engine == "vector":
+                nc.vector.tensor_copy(dst, source)
+            else:
+                nc.scalar.copy(dst, source)
+
+        scale_table = sbuf("scale_table", T, U8)
+        nc.vector.memset(scale_table[:].bitcast(I32), 0)
+        nc.scalar.dma_start(scale_table[0:P:8, :].bitcast(I32), x_scales[0].bitcast(I32))
+
+        offs_t = load_list("offs_t", offs)
+        w1_raw = sbuf("w1_raw", PACK * H, F32, tag="w_raw")
+        nc.sync.dma_start(w1_raw[:], w1.rearrange("(p j) c -> p (j c)", j=PACK))
+        n1_t = load_list("n1_t", n1)
+        n2_t = load_list("n2_t", n2)
+        n3_t = load_list("n3_t", n3)
+        word_table = sbuf("word_table", T, I32)
+        nc.sync.dma_start(word_table[:], x_words[0].rearrange("p c r -> p (c r)").bitcast(I32))
+        n4_t = load_list("n4_t", n4)
+        n5_t = load_list("n5_t", n5)
+
+        tau_t = sbuf("tau_t", 4, F32)
+        with nc.allow_non_contiguous_dma(reason="one rate to a partition and tile"):
+            nc.sync.dma_start(tau_t[:], tau.rearrange("(u p) o -> p (u o)", p=P))
+        gn_t = sbuf("gn_t", PACK, F32)
+        nc.gpsimd.dma_start(gn_t[:], gn.rearrange("(p t) o -> p (t o)", t=PACK))
+        neg_tau = sbuf("neg_tau", 4, F32)
+        nc.gpsimd.tensor_scalar(neg_tau[:], tau_t[:], -1.0, 0.0, ALU.mult, ALU.add)
+
+        picked_scales = sbuf("picked_scales", S, U8)
+        nc.vector.tensor_copy(picked_scales[:], scale_table[:].indirect(offs_t[:]))
+        x_plane = sbuf("x_plane", S, U8)
+        nc.vector.tensor_copy(x_plane[:].bitcast(I32), picked_scales[:].bitcast(I32))
+        for i in range(1, 4):
+            nc.sync.dma_start(x_plane[i:P:32, :].bitcast(I32), picked_scales[8 * i : P : 32, :].bitcast(I32))
+
+        w1_bf = sbuf("w1_bf", PACK * H, BF16)
+        w1_dst = w1_bf[:].rearrange("p (t m j) -> p m j t", t=PACK, j=PACK)
+        w1_src = w1_raw[:].rearrange("p (j m t) -> p m j t", t=PACK, j=PACK)
+        nc.scalar.activation(w1_dst[:, :SCALAR_W1], w1_src[:, :SCALAR_W1], ACT.Copy)
+        nc.vector.tensor_copy(w1_dst[:, SCALAR_W1:], w1_src[:, SCALAR_W1:])
+        w1_codes = sbuf("w1_codes", H, U32)
+        w1_plane = sbuf("w1_plane", H, U8)
+        for t in range(PACK):
+            cols = slice(t * P, (t + 1) * P)
+            nc.vector.quantize_mx(w1_codes[:, cols].bitcast(FP8X4), w1_plane[:, cols], w1_bf[:, t * 512 : (t + 1) * 512])
+
+        w2_raw = sbuf("w2_raw", PACK * N, F32, tag="w_raw")
+        nc.sync.dma_start(w2_raw[:], w2.rearrange("(p t) c -> p (t c)", t=PACK))
+
+        y_bank = [[bank("y%d%d" % (c, q), 2 * c + q) for q in range(2)] for c in range(2)]
+        y_rows = [sbuf("y_rows%d" % t, S, F32) for t in range(PACK)]
+
+        def y_psum(c, t):
+            return y_bank[c][t // 2][:, half(t % 2)]
+
+        for c in range(2):
+            picked_words = sbuf("picked_words%d" % c, HALF, U32)
+            nc.vector.tensor_copy(picked_words[:], word_table[:].bitcast(U32).indirect(list_half(offs_t, c)))
+            for t in (0, 2, 1, 3):
+                cols = slice(t * P, (t + 1) * P)
+                nc.tensor.matmul_mx(
+                    y_psum(c, t),
+                    lhsT=w1_codes[:, cols].bitcast(FP8X4),
+                    lhsT_scale=w1_plane[:, cols],
+                    rhs=picked_words[:].bitcast(FP8X4),
+                    rhs_scale=x_plane[:, half(c)],
+                    start=True,
+                    stop=True,
+                )
+            if c == 0:
+                for t in (0, 2, 1, 3):
+                    nc.scalar.copy(y_rows[t][:, half(0)], y_psum(0, t))
+
+        at1 = [sbuf("at1_%d" % c, PACK * HALF, F32) for c in range(2)]
+        at2 = [sbuf("at2_%d" % c, PACK * HALF, F32) for c in range(2)]
+        at3 = [sbuf("at3_%d" % c, PACK * HALF, F32) for c in range(2)]
+        z_codes = [sbuf("z_codes%d" % c, HALF, U32) for c in range(2)]
+        z_plane = [sbuf("z_plane%d" % c, HALF, U8) for c in range(2)]
+
+        def fetch_y(engine, c, t):
+            for dst, offsets in ((at1, n1_t), (at2, n2_t), (at3, n3_t)):
+                gather(engine, dst[c][:, half(t)], y_rows[t], list_half(offsets, c))
+
+        def combine(c, tiles):
+            for t in tiles:
+                nc.vector.tensor_tensor(at1[c][:, half(t)], y_psum(c, t), at1[c][:, half(t)], ALU.max)
+            for t in tiles:
+                nc.vector.tensor_tensor(at2[c][:, half(t)], at2[c][:, half(t)], at3[c][:, half(t)], ALU.max)
+            for t in tiles:
+                nc.vector.tensor_tensor(at1[c][:, half(t)], at1[c][:, half(t)], at2[c][:, half(t)], ALU.subtract)
+
+        def quantise_z(c):
+            z_bf = sbuf("z_bf%d" % c, PACK * HALF, BF16)
+            nc.vector.tensor_tensor(
+                z_bf[:].rearrange("p (g i t) -> p g t i", i=4, t=PACK),
+                at1[c][:].rearrange("p (t g i) -> p g t i", i=4, t=PACK),
+                gn_t[:].unsqueeze(1).unsqueeze(3).to_broadcast([P, HALF // 4, PACK, 4]),
+                ALU.mult,
+            )
+            nc.vector.quantize_mx(z_codes[c][:].bitcast(FP8X4), z_plane[c][:], z_bf[:])
+
+        w2_codes = sbuf("w2_codes", N, U32)
+        w2_plane = sbuf("w2_plane", N, U8)
+
+        def quantise_w2():
+            w2_bf = sbuf("w2_bf", PACK * N, BF16)
+            nc.vector.tensor_copy(
+                w2_bf[:].rearrange("p (g i t) -> p g t i", i=4, t=PACK),
+                w2_raw[:].rearrange("p (t g i) -> p g t i", i=4, t=PACK),
+            )
+            return w2_bf
+
+        h_first = [bank("h0%d" % q, 4 + q) for q in range(2)]
+        h_second = {}
+
+        def h_psum(c, u):
+            return h_first[u // 2][:, half(u % 2)] if c == 0 else h_second[u][:, half(0)]
+
+        def second_product(c):
+            for u in range(4):
+                if c == 1:
+                    h_second[u] = bank("h1%d" % u, (6 + u) % 8)
+                cols = slice(u * P, (u + 1) * P)
+                nc.tensor.matmul_mx(
+                    h_psum(c, u),
+                    lhsT=w2_codes[:, cols].bitcast(FP8X4),
+                    lhsT_scale=w2_plane[:, cols],
+                    rhs=z_codes[c][:].bitcast(FP8X4),
+                    rhs_scale=z_plane[c][:],
+                    start=True,
+                    stop=True,
+                )
+
+        h_rows = [sbuf("h_rows%d" % u, S, F32) for u in range(4)]
+        sz_rows = [sbuf("sz_rows%d" % u, S, F32) for u in range(4)]
+
+        nc.scalar.copy(y_rows[0][:, half(1)], y_psum(1, 0))
+        nc.vector.tensor_copy(y_rows[2][:, half(1)], y_psum(1, 2))
+        nc.vector.tensor_copy(y_rows[3][:, half(1)], y_psum(1, 3))
+        fetch_y("scalar", 0, 0)
+        fetch_y("vector", 0, 2)
+        nc.scalar.copy(y_rows[1][:, half(1)], y_psum(1, 1))
+        fetch_y("scalar", 0, 1)
+        combine(0, (0, 2))
+        fetch_y("scalar", 0, 3)
+        w2_bf = quantise_w2()
+        combine(0, (1,))
+        nc.vector.quantize_mx(w2_codes[:].bitcast(FP8X4), w2_plane[:], w2_bf[:])
+        combine(0, (3,))
+        quantise_z(0)
+        for t in range(PACK):
+            fetch_y("scalar", 1, t)
+        second_product(0)
+        combine(1, (0, 1))
+        combine(1, (2,))
+        combine(1, (3,))
+        for u in range(4):
+            nc.scalar.activation(sz_rows[u][:, half(0)], h_psum(0, u), ACT.Abs)
+            nc.scalar.copy(h_rows[u][:, half(0)], h_psum(0, u))
+        quantise_z(1)
+        second_product(1)
+
+        ea = [sbuf("ea%d" % u, S, F32) for u in range(4)]
+        res = [sbuf("res%d" % u, S, F32) for u in range(4)]
+
+        def finish_sz(u):
+            nc.scalar.activation(sz_rows[u][:, half(1)], h_psum(1, u), ACT.Abs)
+
+        def finish_h(engine, u):
+            plain_copy(engine, h_rows[u][:, half(1)], h_psum(1, u))
+
+        def fetch_ea(u):
+            for c in range(2):
+                nc.scalar.activation(
+                    ea[u][:, half(c)], sz_rows[u][:].indirect(list_half(n4_t, c)), ACT.Exp, scale=neg_tau[:, u : u + 1]
+                )
+
+        def fetch_h(engine, u, c):
+            gather(engine, res[u][:, half(c)], h_rows[u], list_half(n5_t, c))
+
+        def finish(u):
+            for c in range(2):
+                nc.vector.tensor_tensor(res[u][:, half(c)], h_psum(c, u), res[u][:, half(c)], ALU.subtract)
+            for c in range(2):
+                nc.vector.tensor_tensor(res[u][:, half(c)], res[u][:, half(c)], ea[u][:, half(c)], ALU.mult)
+                nc.sync.dma_start(out[u * P : (u + 1) * P, half(c)], res[u][:, half(c)])
+
+        finish_sz(0)
+        finish_h("vector", 1)
+        finish_h("vector", 0)
+        fetch_ea(0)
+        fetch_h("vector", 0, 0)
+        fetch_h("vector", 0, 1)
+        finish_sz(1)
+        fetch_ea(1)
+        finish(0)
+        finish_sz(2)
+        finish_h("scalar", 2)
+        fetch_h("vector", 1, 0)
+        fetch_h("vector", 1, 1)
+        fetch_ea(2)
+        finish(1)
+        finish_sz(3)
+        finish_h("scalar", 3)
+        fetch_h("vector", 2, 0)
+        fetch_h("vector", 2, 1)
+        fetch_h("scalar", 3, 0)
+        fetch_h("scalar", 3, 1)
+        finish(2)
+        fetch_ea(3)
+        finish(3)

@@ -19,7 +19,8 @@ P = 128
 PACK = 4
 HALF = S // 2
 HALF_COLS = HALF // 16
-SCALAR_W1 = 80
+QUARTER = S // 4
+SCALAR_W1 = 48
 
 
 def tile_picked_hashmixela_none_p_kernel(
@@ -59,18 +60,18 @@ def tile_picked_hashmixela_none_p_kernel(
             else:
                 nc.scalar.copy(dst, source)
 
-        scale_table = sbuf("scale_table", T, U8)
-        nc.vector.memset(scale_table[:].bitcast(I32), 0)
-        nc.scalar.dma_start(scale_table[0:P:8, :].bitcast(I32), x_scales[0].bitcast(I32))
-
         offs_t = load_list("offs_t", offs)
+        scale_table = sbuf("scale_table", T, U8)
+        nc.sync.dma_start(
+            scale_table[:].bitcast(I32), x_scales[0].bitcast(I32).unsqueeze(1).to_broadcast([16, 8, T // 4])
+        )
         w1_raw = sbuf("w1_raw", PACK * H, F32, tag="w_raw")
         nc.sync.dma_start(w1_raw[:], w1.rearrange("(p j) c -> p (j c)", j=PACK))
         n1_t = load_list("n1_t", n1)
         n2_t = load_list("n2_t", n2)
-        n3_t = load_list("n3_t", n3)
         word_table = sbuf("word_table", T, I32)
         nc.sync.dma_start(word_table[:], x_words[0].rearrange("p c r -> p (c r)").bitcast(I32))
+        n3_t = load_list("n3_t", n3)
         n4_t = load_list("n4_t", n4)
         n5_t = load_list("n5_t", n5)
 
@@ -105,84 +106,96 @@ def tile_picked_hashmixela_none_p_kernel(
 
         y_bank = [[bank("y%d%d" % (c, q), 2 * c + q) for q in range(2)] for c in range(2)]
         y_rows = [sbuf("y_rows%d" % t, S, F32) for t in range(PACK)]
+        picked_words = [sbuf("picked_words%d" % c, HALF, U32) for c in range(2)]
+        for c in range(2):
+            nc.vector.tensor_copy(picked_words[c][:], word_table[:].bitcast(U32).indirect(list_half(offs_t, c)))
 
         def y_psum(c, t):
             return y_bank[c][t // 2][:, half(t % 2)]
 
-        for c in range(2):
-            picked_words = sbuf("picked_words%d" % c, HALF, U32)
-            nc.vector.tensor_copy(picked_words[:], word_table[:].bitcast(U32).indirect(list_half(offs_t, c)))
-            for t in (0, 2, 1, 3):
-                cols = slice(t * P, (t + 1) * P)
-                nc.tensor.matmul_mx(
-                    y_psum(c, t),
-                    lhsT=w1_codes[:, cols].bitcast(FP8X4),
-                    lhsT_scale=w1_plane[:, cols],
-                    rhs=picked_words[:].bitcast(FP8X4),
-                    rhs_scale=x_plane[:, half(c)],
-                    start=True,
-                    stop=True,
-                )
-            if c == 0:
-                for t in (0, 2, 1, 3):
-                    nc.scalar.copy(y_rows[t][:, half(0)], y_psum(0, t))
+        def first_product(c, t):
+            cols = slice(t * P, (t + 1) * P)
+            nc.tensor.matmul_mx(
+                y_psum(c, t),
+                lhsT=w1_codes[:, cols].bitcast(FP8X4),
+                lhsT_scale=w1_plane[:, cols],
+                rhs=picked_words[c][:].bitcast(FP8X4),
+                rhs_scale=x_plane[:, half(c)],
+                start=True,
+                stop=True,
+            )
+
+        def keep_y(engine, c, t):
+            plain_copy(engine, y_rows[t][:, half(c)], y_psum(c, t))
 
         at1 = [sbuf("at1_%d" % c, PACK * HALF, F32) for c in range(2)]
         at2 = [sbuf("at2_%d" % c, PACK * HALF, F32) for c in range(2)]
         at3 = [sbuf("at3_%d" % c, PACK * HALF, F32) for c in range(2)]
+        z_bf = [sbuf("z_bf%d" % c, PACK * HALF, BF16) for c in range(2)]
         z_codes = [sbuf("z_codes%d" % c, HALF, U32) for c in range(2)]
         z_plane = [sbuf("z_plane%d" % c, HALF, U8) for c in range(2)]
+        fetched = {1: (at1, n1_t), 2: (at2, n2_t), 3: (at3, n3_t)}
 
-        def fetch_y(engine, c, t):
-            for dst, offsets in ((at1, n1_t), (at2, n2_t), (at3, n3_t)):
-                gather(engine, dst[c][:, half(t)], y_rows[t], list_half(offsets, c))
+        def span(t, first=0, count=HALF):
+            return slice(t * HALF + first, t * HALF + first + count)
 
-        def combine(c, tiles):
-            for t in tiles:
-                nc.vector.tensor_tensor(at1[c][:, half(t)], y_psum(c, t), at1[c][:, half(t)], ALU.max)
-            for t in tiles:
-                nc.vector.tensor_tensor(at2[c][:, half(t)], at2[c][:, half(t)], at3[c][:, half(t)], ALU.max)
-            for t in tiles:
-                nc.vector.tensor_tensor(at1[c][:, half(t)], at1[c][:, half(t)], at2[c][:, half(t)], ALU.subtract)
+        def fetch_y(engine, c, t, lists=(1, 2, 3), first=0, count=HALF):
+            entry = (c * HALF + first) // 16
+            for k in lists:
+                dst, offsets = fetched[k]
+                gather(engine, dst[c][:, span(t, first, count)], y_rows[t], offsets[:, entry : entry + count // 16])
 
-        def quantise_z(c):
-            z_bf = sbuf("z_bf%d" % c, PACK * HALF, BF16)
+        def larger_of_own(c, t, first=0, count=HALF):
+            cols = span(t, first, count)
+            nc.vector.tensor_tensor(at1[c][:, cols], y_bank[c][t // 2][:, span(t % 2, first, count)], at1[c][:, cols], ALU.max)
+
+        def larger_of_others(c, t, first=0, count=HALF):
+            cols = span(t, first, count)
+            nc.vector.tensor_tensor(at2[c][:, cols], at2[c][:, cols], at3[c][:, cols], ALU.max)
+
+        def difference(c, t, first=0, count=HALF):
+            cols = span(t, first, count)
+            nc.vector.tensor_tensor(at1[c][:, cols], at1[c][:, cols], at2[c][:, cols], ALU.subtract)
+
+        def round_z(c, first=0, count=HALF):
+            groups = slice(first // 4, (first + count) // 4)
             nc.vector.tensor_tensor(
-                z_bf[:].rearrange("p (g i t) -> p g t i", i=4, t=PACK),
-                at1[c][:].rearrange("p (t g i) -> p g t i", i=4, t=PACK),
-                gn_t[:].unsqueeze(1).unsqueeze(3).to_broadcast([P, HALF // 4, PACK, 4]),
+                z_bf[c][:].rearrange("p (g i t) -> p g t i", i=4, t=PACK)[:, groups],
+                at1[c][:].rearrange("p (t g i) -> p g t i", i=4, t=PACK)[:, groups],
+                gn_t[:].unsqueeze(1).unsqueeze(3).to_broadcast([P, count // 4, PACK, 4]),
                 ALU.mult,
             )
-            nc.vector.quantize_mx(z_codes[c][:].bitcast(FP8X4), z_plane[c][:], z_bf[:])
+
+        def quantise_z(c, first=0, count=HALF):
+            cols = slice(first, first + count)
+            nc.vector.quantize_mx(
+                z_codes[c][:, cols].bitcast(FP8X4), z_plane[c][:, cols], z_bf[c][:, PACK * first : PACK * (first + count)]
+            )
 
         w2_codes = sbuf("w2_codes", N, U32)
         w2_plane = sbuf("w2_plane", N, U8)
 
-        def quantise_w2():
-            w2_bf = sbuf("w2_bf", PACK * N, BF16)
-            nc.vector.tensor_copy(
-                w2_bf[:].rearrange("p (g i t) -> p g t i", i=4, t=PACK),
-                w2_raw[:].rearrange("p (t g i) -> p g t i", i=4, t=PACK),
-            )
-            return w2_bf
+        w2_bf = sbuf("w2_bf", PACK * N, BF16)
+        w2_dst = w2_bf[:].rearrange("p (m t) -> p m t", t=PACK)
+        w2_src = w2_raw[:].rearrange("p (t m) -> p m t", t=PACK)
+        for c in range(2):
+            part = slice(c * N // 2, (c + 1) * N // 2)
+            nc.gpsimd.tensor_scalar(w2_dst[:, part], w2_src[:, part], 1.0, 0.0, ALU.mult, ALU.add)
 
-        h_first = [bank("h0%d" % q, 4 + q) for q in range(2)]
-        h_second = {}
+        h_bank = [bank("h%d" % u, 4 + u) for u in range(4)]
 
         def h_psum(c, u):
-            return h_first[u // 2][:, half(u % 2)] if c == 0 else h_second[u][:, half(0)]
+            return h_bank[u][:, half(c)]
 
-        def second_product(c):
+        def second_product(c, first=0, count=HALF):
             for u in range(4):
-                if c == 1:
-                    h_second[u] = bank("h1%d" % u, (6 + u) % 8)
                 cols = slice(u * P, (u + 1) * P)
                 nc.tensor.matmul_mx(
-                    h_psum(c, u),
+                    h_bank[u][:, span(c, first, count)],
                     lhsT=w2_codes[:, cols].bitcast(FP8X4),
                     lhsT_scale=w2_plane[:, cols],
-                    rhs=z_codes[c][:].bitcast(FP8X4),
-                    rhs_scale=z_plane[c][:],
+                    rhs=z_codes[c][:, first : first + count].bitcast(FP8X4),
+                    rhs_scale=z_plane[c][:, first : first + count],
                     start=True,
                     stop=True,
                 )
@@ -190,40 +203,74 @@ def tile_picked_hashmixela_none_p_kernel(
         h_rows = [sbuf("h_rows%d" % u, S, F32) for u in range(4)]
         sz_rows = [sbuf("sz_rows%d" % u, S, F32) for u in range(4)]
 
-        nc.scalar.copy(y_rows[0][:, half(1)], y_psum(1, 0))
-        nc.vector.tensor_copy(y_rows[2][:, half(1)], y_psum(1, 2))
-        nc.vector.tensor_copy(y_rows[3][:, half(1)], y_psum(1, 3))
+        for c in range(2):
+            first_product(c, 0)
+            first_product(c, 2)
+            keep_y("scalar", c, 0)
+            keep_y("vector", c, 2)
+        for c in range(2):
+            first_product(c, 1)
+            first_product(c, 3)
         fetch_y("scalar", 0, 0)
         fetch_y("vector", 0, 2)
-        nc.scalar.copy(y_rows[1][:, half(1)], y_psum(1, 1))
+        for c in range(2):
+            keep_y("scalar", c, 1)
+            keep_y("vector", c, 3)
         fetch_y("scalar", 0, 1)
-        combine(0, (0, 2))
-        fetch_y("scalar", 0, 3)
-        w2_bf = quantise_w2()
-        combine(0, (1,))
+        fetch_y("vector", 0, 3, lists=(1, 2))
+        fetch_y("scalar", 0, 3, lists=(3,))
+        larger_of_own(0, 2, 0, 2 * HALF)
+        larger_of_own(0, 0, 0, 2 * HALF)
         nc.vector.quantize_mx(w2_codes[:].bitcast(FP8X4), w2_plane[:], w2_bf[:])
-        combine(0, (3,))
-        quantise_z(0)
-        for t in range(PACK):
+        larger_of_others(0, 0, 0, 2 * HALF)
+        larger_of_others(0, 2, 0, 2 * HALF)
+        difference(0, 0, 0, 2 * HALF)
+        difference(0, 2, 0, 2 * HALF)
+        for t in range(PACK - 1):
             fetch_y("scalar", 1, t)
+        for first in (0, QUARTER):
+            fetch_y("scalar", 1, 3, first=first, count=QUARTER)
+        larger_of_own(1, 0)
+        round_z(0)
+        larger_of_others(1, 0)
+        quantise_z(0)
         second_product(0)
-        combine(1, (0, 1))
-        combine(1, (2,))
-        combine(1, (3,))
+        larger_of_own(1, 1)
+        larger_of_others(1, 1)
+        larger_of_own(1, 2)
+        difference(1, 0, 0, 2 * HALF)
+        larger_of_others(1, 2)
+        larger_of_own(1, 3, 0, QUARTER)
+        larger_of_others(1, 3, 0, QUARTER)
+        difference(1, 2)
+        difference(1, 3, 0, QUARTER)
+        larger_of_own(1, 3, QUARTER, QUARTER)
+        larger_of_others(1, 3, QUARTER, QUARTER)
+        round_z(1, 0, QUARTER)
+        difference(1, 3, QUARTER, QUARTER)
+        quantise_z(1, 0, QUARTER)
+        round_z(1, QUARTER, QUARTER)
+        def keep_sz(u, first, count):
+            cols = slice(first, first + count)
+            nc.scalar.activation(sz_rows[u][:, cols], h_bank[u][:, cols], ACT.Abs)
+
+        def keep_h(engine, u, first, count):
+            cols = slice(first, first + count)
+            plain_copy(engine, h_rows[u][:, cols], h_bank[u][:, cols])
+
         for u in range(4):
-            nc.scalar.activation(sz_rows[u][:, half(0)], h_psum(0, u), ACT.Abs)
-            nc.scalar.copy(h_rows[u][:, half(0)], h_psum(0, u))
-        quantise_z(1)
-        second_product(1)
+            keep_sz(u, 0, HALF)
+            keep_h("scalar", u, 0, HALF)
+        second_product(1, 0, QUARTER)
+        quantise_z(1, QUARTER, QUARTER)
+        for u in range(4):
+            keep_sz(u, HALF, QUARTER)
+            keep_h("scalar", u, HALF, QUARTER)
+        second_product(1, QUARTER, QUARTER)
 
         ea = [sbuf("ea%d" % u, S, F32) for u in range(4)]
         res = [sbuf("res%d" % u, S, F32) for u in range(4)]
-
-        def finish_sz(u):
-            nc.scalar.activation(sz_rows[u][:, half(1)], h_psum(1, u), ACT.Abs)
-
-        def finish_h(engine, u):
-            plain_copy(engine, h_rows[u][:, half(1)], h_psum(1, u))
+        last = HALF + QUARTER
 
         def fetch_ea(u):
             for c in range(2):
@@ -234,34 +281,30 @@ def tile_picked_hashmixela_none_p_kernel(
         def fetch_h(engine, u, c):
             gather(engine, res[u][:, half(c)], h_rows[u], list_half(n5_t, c))
 
-        def finish(u):
+        def less_fetched(u):
             for c in range(2):
-                nc.vector.tensor_tensor(res[u][:, half(c)], h_psum(c, u), res[u][:, half(c)], ALU.subtract)
-            for c in range(2):
-                nc.vector.tensor_tensor(res[u][:, half(c)], res[u][:, half(c)], ea[u][:, half(c)], ALU.mult)
-                nc.sync.dma_start(out[u * P : (u + 1) * P, half(c)], res[u][:, half(c)])
+                nc.vector.tensor_tensor(res[u][:, half(c)], h_bank[u][:, half(c)], res[u][:, half(c)], ALU.subtract)
 
-        finish_sz(0)
-        finish_h("vector", 1)
-        finish_h("vector", 0)
-        fetch_ea(0)
-        fetch_h("vector", 0, 0)
-        fetch_h("vector", 0, 1)
-        finish_sz(1)
-        fetch_ea(1)
-        finish(0)
-        finish_sz(2)
-        finish_h("scalar", 2)
-        fetch_h("vector", 1, 0)
-        fetch_h("vector", 1, 1)
-        fetch_ea(2)
-        finish(1)
-        finish_sz(3)
-        finish_h("scalar", 3)
-        fetch_h("vector", 2, 0)
-        fetch_h("vector", 2, 1)
-        fetch_h("scalar", 3, 0)
-        fetch_h("scalar", 3, 1)
-        finish(2)
-        fetch_ea(3)
-        finish(3)
+        def finish(u):
+            rows = slice(u * P, (u + 1) * P)
+            engine, queue = (nc.gpsimd, nc.sync) if u < 3 else (nc.vector, nc.scalar)
+            for c in range(2):
+                engine.tensor_tensor(res[u][:, half(c)], res[u][:, half(c)], ea[u][:, half(c)], ALU.mult)
+                queue.dma_start(out[rows, half(c)], res[u][:, half(c)])
+
+        keep_h("vector", 0, last, QUARTER)
+        keep_sz(1, last, QUARTER)
+        keep_sz(0, last, QUARTER)
+        keep_h("vector", 1, last, QUARTER)
+        for u in range(4):
+            fetch_h("vector", u, 0)
+            if u < 3:
+                fetch_h("vector", u, 1)
+            fetch_ea(u)
+            if u < 2:
+                keep_h("scalar", u + 2, last, QUARTER)
+                keep_sz(u + 2, last, QUARTER)
+            if u == 1:
+                fetch_h("scalar", 3, 1)
+            less_fetched(u)
+            finish(u)

@@ -20,7 +20,6 @@ PACK = 4
 HALF = S // 2
 HALF_COLS = HALF // 16
 QUARTER = S // 4
-SCALAR_W1 = 48
 
 
 def tile_picked_hashmixela_none_p_kernel(
@@ -60,18 +59,18 @@ def tile_picked_hashmixela_none_p_kernel(
             else:
                 nc.scalar.copy(dst, source)
 
-        offs_t = load_list("offs_t", offs)
         scale_table = sbuf("scale_table", T, U8)
-        nc.sync.dma_start(
-            scale_table[:].bitcast(I32), x_scales[0].bitcast(I32).unsqueeze(1).to_broadcast([16, 8, T // 4])
-        )
-        w1_raw = sbuf("w1_raw", PACK * H, F32, tag="w_raw")
-        nc.sync.dma_start(w1_raw[:], w1.rearrange("(p j) c -> p (j c)", j=PACK))
+        nc.gpsimd.memset(scale_table[:].bitcast(U32), 0)
+        nc.scalar.dma_start(scale_table[0:P:8, :].bitcast(I32), x_scales[0].bitcast(I32))
+
+        offs_t = load_list("offs_t", offs)
         n1_t = load_list("n1_t", n1)
         n2_t = load_list("n2_t", n2)
+        n3_t = load_list("n3_t", n3)
+        w1_raw = sbuf("w1_raw", PACK * H, F32, tag="w_raw")
+        nc.sync.dma_start(w1_raw[:], w1.rearrange("(p j) c -> p (j c)", j=PACK))
         word_table = sbuf("word_table", T, I32)
         nc.sync.dma_start(word_table[:], x_words[0].rearrange("p c r -> p (c r)").bitcast(I32))
-        n3_t = load_list("n3_t", n3)
         n4_t = load_list("n4_t", n4)
         n5_t = load_list("n5_t", n5)
 
@@ -83,6 +82,9 @@ def tile_picked_hashmixela_none_p_kernel(
         neg_tau = sbuf("neg_tau", 4, F32)
         nc.gpsimd.tensor_scalar(neg_tau[:], tau_t[:], -1.0, 0.0, ALU.mult, ALU.add)
 
+        neg_gn = sbuf("neg_gn", PACK, F32)
+        nc.gpsimd.tensor_scalar(neg_gn[:], gn_t[:], -1.0, 0.0, ALU.mult, ALU.add)
+
         picked_scales = sbuf("picked_scales", S, U8)
         nc.vector.tensor_copy(picked_scales[:], scale_table[:].indirect(offs_t[:]))
         x_plane = sbuf("x_plane", S, U8)
@@ -91,13 +93,14 @@ def tile_picked_hashmixela_none_p_kernel(
             nc.sync.dma_start(x_plane[i:P:32, :].bitcast(I32), picked_scales[8 * i : P : 32, :].bitcast(I32))
 
         w1_bf = sbuf("w1_bf", PACK * H, BF16)
-        w1_dst = w1_bf[:].rearrange("p (t m j) -> p m j t", t=PACK, j=PACK)
-        w1_src = w1_raw[:].rearrange("p (j m t) -> p m j t", t=PACK, j=PACK)
-        nc.scalar.activation(w1_dst[:, :SCALAR_W1], w1_src[:, :SCALAR_W1], ACT.Copy)
-        nc.vector.tensor_copy(w1_dst[:, SCALAR_W1:], w1_src[:, SCALAR_W1:])
+        w1_dst = w1_bf[:].rearrange("p (t m j) -> p t m j", t=PACK, j=PACK)
+        w1_src = w1_raw[:].rearrange("p (j m t) -> p t m j", t=PACK, j=PACK)
         w1_codes = sbuf("w1_codes", H, U32)
         w1_plane = sbuf("w1_plane", H, U8)
-        for t in range(PACK):
+        for t in (0, 1):
+            nc.scalar.activation(w1_dst[:, t], w1_src[:, t], ACT.Copy)
+            nc.vector.tensor_copy(w1_dst[:, t + 2], w1_src[:, t + 2])
+        for t in (2, 0, 3, 1):
             cols = slice(t * P, (t + 1) * P)
             nc.vector.quantize_mx(w1_codes[:, cols].bitcast(FP8X4), w1_plane[:, cols], w1_bf[:, t * 512 : (t + 1) * 512])
 
@@ -132,6 +135,7 @@ def tile_picked_hashmixela_none_p_kernel(
         at2 = [sbuf("at2_%d" % c, PACK * HALF, F32) for c in range(2)]
         at3 = [sbuf("at3_%d" % c, PACK * HALF, F32) for c in range(2)]
         z_bf = [sbuf("z_bf%d" % c, PACK * HALF, BF16) for c in range(2)]
+        z_rows = [sbuf("z_rows%d" % c, PACK * HALF, BF16) for c in range(2)]
         z_codes = [sbuf("z_codes%d" % c, HALF, U32) for c in range(2)]
         z_plane = [sbuf("z_plane%d" % c, HALF, U8) for c in range(2)]
         fetched = {1: (at1, n1_t), 2: (at2, n2_t), 3: (at3, n3_t)}
@@ -153,17 +157,21 @@ def tile_picked_hashmixela_none_p_kernel(
             cols = span(t, first, count)
             nc.vector.tensor_tensor(at2[c][:, cols], at2[c][:, cols], at3[c][:, cols], ALU.max)
 
+        def gain(c, t, first=0, count=HALF):
+            cols = span(t, first, count)
+            nc.vector.tensor_scalar(at1[c][:, cols], at1[c][:, cols], gn_t[:, t : t + 1], None, ALU.mult)
+
         def difference(c, t, first=0, count=HALF):
             cols = span(t, first, count)
-            nc.vector.tensor_tensor(at1[c][:, cols], at1[c][:, cols], at2[c][:, cols], ALU.subtract)
+            nc.vector.scalar_tensor_tensor(
+                z_rows[c][:, cols], at2[c][:, cols], neg_gn[:, t : t + 1], at1[c][:, cols], ALU.mult, ALU.add
+            )
 
-        def round_z(c, first=0, count=HALF):
-            groups = slice(first // 4, (first + count) // 4)
-            nc.vector.tensor_tensor(
-                z_bf[c][:].rearrange("p (g i t) -> p g t i", i=4, t=PACK)[:, groups],
-                at1[c][:].rearrange("p (t g i) -> p g t i", i=4, t=PACK)[:, groups],
-                gn_t[:].unsqueeze(1).unsqueeze(3).to_broadcast([P, count // 4, PACK, 4]),
-                ALU.mult,
+        def weave_z(c, first=0, count=HALF):
+            cols = slice(first, first + count)
+            nc.vector.tensor_copy(
+                z_bf[c][:].rearrange("p (j t) -> p j t", t=PACK)[:, cols],
+                z_rows[c][:].rearrange("p (t j) -> p j t", t=PACK)[:, cols],
             )
 
         def quantise_z(c, first=0, count=HALF):
@@ -222,34 +230,43 @@ def tile_picked_hashmixela_none_p_kernel(
         larger_of_own(0, 2, 0, 2 * HALF)
         larger_of_own(0, 0, 0, 2 * HALF)
         nc.vector.quantize_mx(w2_codes[:].bitcast(FP8X4), w2_plane[:], w2_bf[:])
+        for t in (2, 3, 0, 1):
+            gain(0, t)
         larger_of_others(0, 0, 0, 2 * HALF)
         larger_of_others(0, 2, 0, 2 * HALF)
-        difference(0, 0, 0, 2 * HALF)
-        difference(0, 2, 0, 2 * HALF)
+        for t in range(PACK):
+            difference(0, t)
         for t in range(PACK - 1):
             fetch_y("scalar", 1, t)
         for first in (0, QUARTER):
             fetch_y("scalar", 1, 3, first=first, count=QUARTER)
         larger_of_own(1, 0)
-        round_z(0)
+        weave_z(0)
         larger_of_others(1, 0)
         quantise_z(0)
         second_product(0)
+        gain(1, 0)
         larger_of_own(1, 1)
+        difference(1, 0)
         larger_of_others(1, 1)
+        gain(1, 1)
         larger_of_own(1, 2)
-        difference(1, 0, 0, 2 * HALF)
+        difference(1, 1)
         larger_of_others(1, 2)
+        gain(1, 2)
         larger_of_own(1, 3, 0, QUARTER)
-        larger_of_others(1, 3, 0, QUARTER)
         difference(1, 2)
-        difference(1, 3, 0, QUARTER)
+        gain(1, 3, 0, QUARTER)
+        larger_of_others(1, 3, 0, QUARTER)
         larger_of_own(1, 3, QUARTER, QUARTER)
+        difference(1, 3, 0, QUARTER)
+        gain(1, 3, QUARTER, QUARTER)
+        weave_z(1, 0, QUARTER)
         larger_of_others(1, 3, QUARTER, QUARTER)
-        round_z(1, 0, QUARTER)
-        difference(1, 3, QUARTER, QUARTER)
         quantise_z(1, 0, QUARTER)
-        round_z(1, QUARTER, QUARTER)
+        difference(1, 3, QUARTER, QUARTER)
+        weave_z(1, QUARTER, QUARTER)
+
         def keep_sz(u, first, count):
             cols = slice(first, first + count)
             nc.scalar.activation(sz_rows[u][:, cols], h_bank[u][:, cols], ACT.Abs)

@@ -17,9 +17,14 @@ ACT = mybir.ActivationFunctionType
 
 P = 128
 PACK = 4
+ROW_TILES = N // P
+BANK = 512
+PER_COLUMN = 16
 HALF = S // 2
-HALF_COLS = HALF // 16
 QUARTER = S // 4
+LAST = S - QUARTER
+H_PIECES = ((0, HALF), (HALF, QUARTER), (LAST, QUARTER))
+SCALAR_W1 = 48
 
 
 def tile_picked_hashmixela_none_p_kernel(
@@ -34,18 +39,18 @@ def tile_picked_hashmixela_none_p_kernel(
             return keep.tile([P, cols], dtype, name=name, tag=tag or name, align_bytes=64)
 
         def bank(name, number):
-            return psum.tile([P, 512], F32, name=name, tag="bank%d" % number)
+            return psum.tile([P, BANK], F32, name=name, tag="bank%d" % number)
 
         def load_list(name, source):
-            tile = sbuf(name, S // 16, U16)
+            tile = sbuf(name, S // PER_COLUMN, U16)
             nc.sync.dma_start(tile[:], source)
             return tile
 
-        def half(c):
-            return slice(c * HALF, (c + 1) * HALF)
+        def span(index, first=0, count=HALF):
+            return slice(index * HALF + first, index * HALF + first + count)
 
-        def list_half(tile, c):
-            return tile[:, c * HALF_COLS : (c + 1) * HALF_COLS]
+        def entries(list_tile, first, count):
+            return list_tile[:, first // PER_COLUMN : (first + count) // PER_COLUMN]
 
         def gather(engine, dst, window, offsets):
             if engine == "vector":
@@ -59,29 +64,28 @@ def tile_picked_hashmixela_none_p_kernel(
             else:
                 nc.scalar.copy(dst, source)
 
-        scale_table = sbuf("scale_table", T, U8)
-        nc.gpsimd.memset(scale_table[:].bitcast(U32), 0)
-        nc.scalar.dma_start(scale_table[0:P:8, :].bitcast(I32), x_scales[0].bitcast(I32))
-
         offs_t = load_list("offs_t", offs)
-        n1_t = load_list("n1_t", n1)
-        n2_t = load_list("n2_t", n2)
-        n3_t = load_list("n3_t", n3)
+        scale_table = sbuf("scale_table", T, U8)
+        nc.sync.dma_start(
+            scale_table[:].bitcast(I32), x_scales[0].bitcast(I32).unsqueeze(1).to_broadcast([16, 8, T // 4])
+        )
         w1_raw = sbuf("w1_raw", PACK * H, F32, tag="w_raw")
         nc.sync.dma_start(w1_raw[:], w1.rearrange("(p j) c -> p (j c)", j=PACK))
+        n1_t = load_list("n1_t", n1)
+        n2_t = load_list("n2_t", n2)
         word_table = sbuf("word_table", T, I32)
         nc.sync.dma_start(word_table[:], x_words[0].rearrange("p c r -> p (c r)").bitcast(I32))
+        n3_t = load_list("n3_t", n3)
         n4_t = load_list("n4_t", n4)
         n5_t = load_list("n5_t", n5)
 
-        tau_t = sbuf("tau_t", 4, F32)
+        tau_t = sbuf("tau_t", ROW_TILES, F32)
         with nc.allow_non_contiguous_dma(reason="one rate to a partition and tile"):
             nc.sync.dma_start(tau_t[:], tau.rearrange("(u p) o -> p (u o)", p=P))
         gn_t = sbuf("gn_t", PACK, F32)
         nc.gpsimd.dma_start(gn_t[:], gn.rearrange("(p t) o -> p (t o)", t=PACK))
-        neg_tau = sbuf("neg_tau", 4, F32)
+        neg_tau = sbuf("neg_tau", ROW_TILES, F32)
         nc.gpsimd.tensor_scalar(neg_tau[:], tau_t[:], -1.0, 0.0, ALU.mult, ALU.add)
-
         neg_gn = sbuf("neg_gn", PACK, F32)
         nc.gpsimd.tensor_scalar(neg_gn[:], gn_t[:], -1.0, 0.0, ALU.mult, ALU.add)
 
@@ -89,20 +93,21 @@ def tile_picked_hashmixela_none_p_kernel(
         nc.vector.tensor_copy(picked_scales[:], scale_table[:].indirect(offs_t[:]))
         x_plane = sbuf("x_plane", S, U8)
         nc.vector.tensor_copy(x_plane[:].bitcast(I32), picked_scales[:].bitcast(I32))
-        for i in range(1, 4):
-            nc.sync.dma_start(x_plane[i:P:32, :].bitcast(I32), picked_scales[8 * i : P : 32, :].bitcast(I32))
+        for r in range(1, 4):
+            nc.sync.dma_start(x_plane[r:P:32, :].bitcast(I32), picked_scales[8 * r : P : 32, :].bitcast(I32))
 
         w1_bf = sbuf("w1_bf", PACK * H, BF16)
-        w1_dst = w1_bf[:].rearrange("p (t m j) -> p t m j", t=PACK, j=PACK)
-        w1_src = w1_raw[:].rearrange("p (j m t) -> p t m j", t=PACK, j=PACK)
+        w1_dst = w1_bf[:].rearrange("p (t m j) -> p m j t", t=PACK, j=PACK)
+        w1_src = w1_raw[:].rearrange("p (j m t) -> p m j t", t=PACK, j=PACK)
+        nc.scalar.activation(w1_dst[:, :SCALAR_W1], w1_src[:, :SCALAR_W1], ACT.Copy)
+        nc.vector.tensor_copy(w1_dst[:, SCALAR_W1:], w1_src[:, SCALAR_W1:])
         w1_codes = sbuf("w1_codes", H, U32)
         w1_plane = sbuf("w1_plane", H, U8)
-        for t in (0, 1):
-            nc.scalar.activation(w1_dst[:, t], w1_src[:, t], ACT.Copy)
-            nc.vector.tensor_copy(w1_dst[:, t + 2], w1_src[:, t + 2])
-        for t in (2, 0, 3, 1):
+        for t in range(PACK):
             cols = slice(t * P, (t + 1) * P)
-            nc.vector.quantize_mx(w1_codes[:, cols].bitcast(FP8X4), w1_plane[:, cols], w1_bf[:, t * 512 : (t + 1) * 512])
+            nc.vector.quantize_mx(
+                w1_codes[:, cols].bitcast(FP8X4), w1_plane[:, cols], w1_bf[:, PACK * t * P : PACK * (t + 1) * P]
+            )
 
         w2_raw = sbuf("w2_raw", PACK * N, F32, tag="w_raw")
         nc.sync.dma_start(w2_raw[:], w2.rearrange("(p t) c -> p (t c)", t=PACK))
@@ -111,10 +116,12 @@ def tile_picked_hashmixela_none_p_kernel(
         y_rows = [sbuf("y_rows%d" % t, S, F32) for t in range(PACK)]
         picked_words = [sbuf("picked_words%d" % c, HALF, U32) for c in range(2)]
         for c in range(2):
-            nc.vector.tensor_copy(picked_words[c][:], word_table[:].bitcast(U32).indirect(list_half(offs_t, c)))
+            nc.vector.tensor_copy(
+                picked_words[c][:], word_table[:].bitcast(U32).indirect(entries(offs_t, c * HALF, HALF))
+            )
 
-        def y_psum(c, t):
-            return y_bank[c][t // 2][:, half(t % 2)]
+        def y_psum(c, t, first=0, count=HALF):
+            return y_bank[c][t // 2][:, span(t % 2, first, count)]
 
         def first_product(c, t):
             cols = slice(t * P, (t + 1) * P)
@@ -123,35 +130,30 @@ def tile_picked_hashmixela_none_p_kernel(
                 lhsT=w1_codes[:, cols].bitcast(FP8X4),
                 lhsT_scale=w1_plane[:, cols],
                 rhs=picked_words[c][:].bitcast(FP8X4),
-                rhs_scale=x_plane[:, half(c)],
+                rhs_scale=x_plane[:, span(c)],
                 start=True,
                 stop=True,
             )
 
         def keep_y(engine, c, t):
-            plain_copy(engine, y_rows[t][:, half(c)], y_psum(c, t))
+            plain_copy(engine, y_rows[t][:, span(c)], y_psum(c, t))
 
         at1 = [sbuf("at1_%d" % c, PACK * HALF, F32) for c in range(2)]
         at2 = [sbuf("at2_%d" % c, PACK * HALF, F32) for c in range(2)]
         at3 = [sbuf("at3_%d" % c, PACK * HALF, F32) for c in range(2)]
-        z_bf = [sbuf("z_bf%d" % c, PACK * HALF, BF16) for c in range(2)]
+        z_woven = [sbuf("z_woven%d" % c, PACK * HALF, BF16) for c in range(2)]
         z_rows = [sbuf("z_rows%d" % c, PACK * HALF, BF16) for c in range(2)]
         z_codes = [sbuf("z_codes%d" % c, HALF, U32) for c in range(2)]
         z_plane = [sbuf("z_plane%d" % c, HALF, U8) for c in range(2)]
-        fetched = {1: (at1, n1_t), 2: (at2, n2_t), 3: (at3, n3_t)}
 
-        def span(t, first=0, count=HALF):
-            return slice(t * HALF + first, t * HALF + first + count)
-
-        def fetch_y(engine, c, t, lists=(1, 2, 3), first=0, count=HALF):
-            entry = (c * HALF + first) // 16
-            for k in lists:
-                dst, offsets = fetched[k]
-                gather(engine, dst[c][:, span(t, first, count)], y_rows[t], offsets[:, entry : entry + count // 16])
+        def fetch_y(engine, c, t, first=0, count=HALF):
+            for dst, list_tile in ((at1, n1_t), (at2, n2_t), (at3, n3_t)):
+                offsets = entries(list_tile, c * HALF + first, count)
+                gather(engine, dst[c][:, span(t, first, count)], y_rows[t], offsets)
 
         def larger_of_own(c, t, first=0, count=HALF):
             cols = span(t, first, count)
-            nc.vector.tensor_tensor(at1[c][:, cols], y_bank[c][t // 2][:, span(t % 2, first, count)], at1[c][:, cols], ALU.max)
+            nc.vector.tensor_tensor(at1[c][:, cols], y_psum(c, t, first, count), at1[c][:, cols], ALU.max)
 
         def larger_of_others(c, t, first=0, count=HALF):
             cols = span(t, first, count)
@@ -170,36 +172,42 @@ def tile_picked_hashmixela_none_p_kernel(
         def weave_z(c, first=0, count=HALF):
             cols = slice(first, first + count)
             nc.vector.tensor_copy(
-                z_bf[c][:].rearrange("p (j t) -> p j t", t=PACK)[:, cols],
+                z_woven[c][:].rearrange("p (j t) -> p j t", t=PACK)[:, cols],
                 z_rows[c][:].rearrange("p (t j) -> p j t", t=PACK)[:, cols],
             )
 
         def quantise_z(c, first=0, count=HALF):
             cols = slice(first, first + count)
             nc.vector.quantize_mx(
-                z_codes[c][:, cols].bitcast(FP8X4), z_plane[c][:, cols], z_bf[c][:, PACK * first : PACK * (first + count)]
+                z_codes[c][:, cols].bitcast(FP8X4),
+                z_plane[c][:, cols],
+                z_woven[c][:, PACK * first : PACK * (first + count)],
             )
 
         w2_codes = sbuf("w2_codes", N, U32)
         w2_plane = sbuf("w2_plane", N, U8)
-
         w2_bf = sbuf("w2_bf", PACK * N, BF16)
         w2_dst = w2_bf[:].rearrange("p (m t) -> p m t", t=PACK)
         w2_src = w2_raw[:].rearrange("p (t m) -> p m t", t=PACK)
-        for c in range(2):
-            part = slice(c * N // 2, (c + 1) * N // 2)
-            nc.gpsimd.tensor_scalar(w2_dst[:, part], w2_src[:, part], 1.0, 0.0, ALU.mult, ALU.add)
+        for first in (0, N // 2):
+            cols = slice(first, first + N // 2)
+            nc.gpsimd.tensor_scalar(w2_dst[:, cols], w2_src[:, cols], 1.0, 0.0, ALU.mult, ALU.add)
 
-        h_bank = [bank("h%d" % u, 4 + u) for u in range(4)]
+        h_bank = [bank("h%d" % u, 4 + u) for u in range(ROW_TILES)]
+        h_last = {}
 
-        def h_psum(c, u):
-            return h_bank[u][:, half(c)]
+        def h_psum(u, first, count):
+            if first < LAST:
+                return h_bank[u][:, first : first + count]
+            return h_last[u][:, :count]
 
         def second_product(c, first=0, count=HALF):
-            for u in range(4):
+            for u in range(ROW_TILES):
+                if c * HALF + first == LAST:
+                    h_last[u] = bank("h_last%d" % u, u)
                 cols = slice(u * P, (u + 1) * P)
                 nc.tensor.matmul_mx(
-                    h_bank[u][:, span(c, first, count)],
+                    h_psum(u, c * HALF + first, count),
                     lhsT=w2_codes[:, cols].bitcast(FP8X4),
                     lhsT_scale=w2_plane[:, cols],
                     rhs=z_codes[c][:, first : first + count].bitcast(FP8X4),
@@ -208,8 +216,14 @@ def tile_picked_hashmixela_none_p_kernel(
                     stop=True,
                 )
 
-        h_rows = [sbuf("h_rows%d" % u, S, F32) for u in range(4)]
-        sz_rows = [sbuf("sz_rows%d" % u, S, F32) for u in range(4)]
+        h_rows = [sbuf("h_rows%d" % u, S, F32) for u in range(ROW_TILES)]
+        sz_rows = [sbuf("sz_rows%d" % u, S, F32) for u in range(ROW_TILES)]
+
+        def keep_sz(u, first, count):
+            nc.scalar.activation(sz_rows[u][:, first : first + count], h_psum(u, first, count), ACT.Abs)
+
+        def keep_h(engine, u, first, count):
+            plain_copy(engine, h_rows[u][:, first : first + count], h_psum(u, first, count))
 
         for c in range(2):
             first_product(c, 0)
@@ -225,103 +239,96 @@ def tile_picked_hashmixela_none_p_kernel(
             keep_y("scalar", c, 1)
             keep_y("vector", c, 3)
         fetch_y("scalar", 0, 1)
-        fetch_y("vector", 0, 3, lists=(1, 2))
-        fetch_y("scalar", 0, 3, lists=(3,))
-        larger_of_own(0, 2, 0, 2 * HALF)
-        larger_of_own(0, 0, 0, 2 * HALF)
+        fetch_y("vector", 0, 3)
+        for t in (2, 0):
+            larger_of_own(0, t, 0, 2 * HALF)
         nc.vector.quantize_mx(w2_codes[:].bitcast(FP8X4), w2_plane[:], w2_bf[:])
         for t in (2, 3, 0, 1):
             gain(0, t)
-        larger_of_others(0, 0, 0, 2 * HALF)
-        larger_of_others(0, 2, 0, 2 * HALF)
+        for t in (2, 0):
+            larger_of_others(0, t, 0, 2 * HALF)
         for t in range(PACK):
             difference(0, t)
-        for t in range(PACK - 1):
-            fetch_y("scalar", 1, t)
-        for first in (0, QUARTER):
-            fetch_y("scalar", 1, 3, first=first, count=QUARTER)
-        larger_of_own(1, 0)
+
+        pieces = [(t, 0, HALF) for t in range(PACK - 1)] + [(PACK - 1, 0, QUARTER), (PACK - 1, QUARTER, QUARTER)]
+        for piece in pieces:
+            fetch_y("scalar", 1, *piece)
+        larger_of_own(1, *pieces[0])
         weave_z(0)
-        larger_of_others(1, 0)
+        larger_of_others(1, *pieces[0])
         quantise_z(0)
         second_product(0)
-        gain(1, 0)
-        larger_of_own(1, 1)
-        difference(1, 0)
-        larger_of_others(1, 1)
-        gain(1, 1)
-        larger_of_own(1, 2)
-        difference(1, 1)
-        larger_of_others(1, 2)
-        gain(1, 2)
-        larger_of_own(1, 3, 0, QUARTER)
-        difference(1, 2)
-        gain(1, 3, 0, QUARTER)
-        larger_of_others(1, 3, 0, QUARTER)
-        larger_of_own(1, 3, QUARTER, QUARTER)
-        difference(1, 3, 0, QUARTER)
-        gain(1, 3, QUARTER, QUARTER)
+        gain(1, *pieces[0])
+        for done, piece in zip(pieces[:3], pieces[1:4]):
+            larger_of_own(1, *piece)
+            difference(1, *done)
+            gain(1, *piece)
+            larger_of_others(1, *piece)
+        larger_of_own(1, *pieces[4])
+        difference(1, *pieces[3])
+        gain(1, *pieces[4])
         weave_z(1, 0, QUARTER)
-        larger_of_others(1, 3, QUARTER, QUARTER)
+        larger_of_others(1, *pieces[4])
         quantise_z(1, 0, QUARTER)
-        difference(1, 3, QUARTER, QUARTER)
+        difference(1, *pieces[4])
         weave_z(1, QUARTER, QUARTER)
 
-        def keep_sz(u, first, count):
-            cols = slice(first, first + count)
-            nc.scalar.activation(sz_rows[u][:, cols], h_bank[u][:, cols], ACT.Abs)
-
-        def keep_h(engine, u, first, count):
-            cols = slice(first, first + count)
-            plain_copy(engine, h_rows[u][:, cols], h_bank[u][:, cols])
-
-        for u in range(4):
+        for u in range(ROW_TILES):
             keep_sz(u, 0, HALF)
             keep_h("scalar", u, 0, HALF)
         second_product(1, 0, QUARTER)
         quantise_z(1, QUARTER, QUARTER)
-        for u in range(4):
+        for u in range(ROW_TILES):
             keep_sz(u, HALF, QUARTER)
             keep_h("scalar", u, HALF, QUARTER)
         second_product(1, QUARTER, QUARTER)
 
-        ea = [sbuf("ea%d" % u, S, F32) for u in range(4)]
-        res = [sbuf("res%d" % u, S, F32) for u in range(4)]
-        last = HALF + QUARTER
+        ea = [sbuf("ea%d" % u, S, F32) for u in range(ROW_TILES)]
+        res = [sbuf("res%d" % u, S, F32) for u in range(ROW_TILES)]
 
-        def fetch_ea(u):
-            for c in range(2):
-                nc.scalar.activation(
-                    ea[u][:, half(c)], sz_rows[u][:].indirect(list_half(n4_t, c)), ACT.Exp, scale=neg_tau[:, u : u + 1]
-                )
+        def fetch_ea(u, first, count=HALF):
+            nc.scalar.activation(
+                ea[u][:, first : first + count],
+                sz_rows[u][:].indirect(entries(n4_t, first, count)),
+                ACT.Exp,
+                scale=neg_tau[:, u : u + 1],
+            )
 
         def fetch_h(engine, u, c):
-            gather(engine, res[u][:, half(c)], h_rows[u], list_half(n5_t, c))
+            gather(engine, res[u][:, span(c)], h_rows[u], entries(n5_t, c * HALF, HALF))
 
         def less_fetched(u):
-            for c in range(2):
-                nc.vector.tensor_tensor(res[u][:, half(c)], h_bank[u][:, half(c)], res[u][:, half(c)], ALU.subtract)
+            for first, count in H_PIECES:
+                cols = slice(first, first + count)
+                nc.vector.tensor_tensor(res[u][:, cols], h_psum(u, first, count), res[u][:, cols], ALU.subtract)
 
-        def finish(u):
-            rows = slice(u * P, (u + 1) * P)
-            engine, queue = (nc.gpsimd, nc.sync) if u < 3 else (nc.vector, nc.scalar)
-            for c in range(2):
-                engine.tensor_tensor(res[u][:, half(c)], res[u][:, half(c)], ea[u][:, half(c)], ALU.mult)
-                queue.dma_start(out[rows, half(c)], res[u][:, half(c)])
+        def finish(engine, queue, u, first, count=HALF):
+            cols = slice(first, first + count)
+            engine.tensor_tensor(res[u][:, cols], res[u][:, cols], ea[u][:, cols], ALU.mult)
+            queue.dma_start(out[u * P : (u + 1) * P, cols], res[u][:, cols])
 
-        keep_h("vector", 0, last, QUARTER)
-        keep_sz(1, last, QUARTER)
-        keep_sz(0, last, QUARTER)
-        keep_h("vector", 1, last, QUARTER)
-        for u in range(4):
-            fetch_h("vector", u, 0)
-            if u < 3:
-                fetch_h("vector", u, 1)
-            fetch_ea(u)
-            if u < 2:
-                keep_h("scalar", u + 2, last, QUARTER)
-                keep_sz(u + 2, last, QUARTER)
-            if u == 1:
-                fetch_h("scalar", 3, 1)
+        keep_h("vector", 0, LAST, QUARTER)
+        keep_sz(1, LAST, QUARTER)
+        keep_sz(0, LAST, QUARTER)
+        keep_h("vector", 1, LAST, QUARTER)
+        final = ROW_TILES - 1
+        for u in range(final):
+            for c in range(2):
+                fetch_h("vector", u, c)
+            for c in range(2):
+                fetch_ea(u, c * HALF)
+            if u + 2 < ROW_TILES:
+                keep_h("vector", u + 2, LAST, QUARTER)
+                keep_sz(u + 2, LAST, QUARTER)
+            if u > 0:
+                fetch_h("scalar", final, u - 1)
             less_fetched(u)
-            finish(u)
+            finish(nc.gpsimd, nc.sync, u, 0)
+            if u < final - 1:
+                finish(nc.gpsimd, nc.sync, u, HALF)
+        for first, count in H_PIECES:
+            fetch_ea(final, first, count)
+        less_fetched(final)
+        finish(nc.vector, nc.scalar, final - 1, HALF)
+        for first, count in H_PIECES:
+            finish(nc.vector, nc.scalar, final, first, count)

from contextlib import ExitStack

import concourse.mybir as mybir

K, T, S, N, H = 512, 2048, 512, 512, 512
FLOPS = 2 * K * H * S + 2 * H * N * S

F32 = mybir.dt.float32
BF16 = mybir.dt.bfloat16
I32 = mybir.dt.int32
U32 = mybir.dt.uint32
U16 = mybir.dt.uint16
U8 = mybir.dt.uint8
FP8X4 = mybir.dt.float8_e4m3fn_x4
ALU = mybir.AluOpType
ACT = mybir.ActivationFunctionType

P = 128
PACK = 4
ROW_TILES = N // P
BANK = 512
PER_COLUMN = 16
HALF = S // 2
QUARTER = S // 4
LAST = S - QUARTER
H_PIECES = ((0, HALF), (HALF, QUARTER), (LAST, QUARTER))
SCALAR_W1 = 48


def tile_picked_hashmixela_none_p_kernel(
    tc, x_words, x_scales, w1, gn, w2, tau, offs, n1, n2, n3, n4, n5, out
):
    nc = tc.nc
    with ExitStack() as ctx:
        keep = ctx.enter_context(tc.tile_pool(name="keep", bufs=1))
        psum = ctx.enter_context(tc.psum_pool(name="psum", bufs=1))

        def sbuf(name, cols, dtype, tag=""):
            return keep.tile([P, cols], dtype, name=name, tag=tag or name, align_bytes=64)

        def bank(name, number):
            return psum.tile([P, BANK], F32, name=name, tag="bank%d" % number)

        def load_list(name, source):
            tile = sbuf(name, S // PER_COLUMN, U16)
            nc.sync.dma_start(tile[:], source)
            return tile

        def span(index, first=0, count=HALF):
            return slice(index * HALF + first, index * HALF + first + count)

        def entries(list_tile, first, count):
            return list_tile[:, first // PER_COLUMN : (first + count) // PER_COLUMN]

        def gather(engine, dst, window, offsets):
            if engine == "vector":
                nc.vector.tensor_copy(dst, window[:].indirect(offsets))
            else:
                nc.scalar.activation(dst, window[:].indirect(offsets), ACT.Copy)

        def plain_copy(engine, dst, source):
            if engine == "vector":
                nc.vector.tensor_copy(dst, source)
            else:
                nc.scalar.copy(dst, source)

        offs_t = load_list("offs_t", offs)
        scale_table = sbuf("scale_table", T, U8)
        nc.sync.dma_start(
            scale_table[:].bitcast(I32), x_scales[0].bitcast(I32).unsqueeze(1).to_broadcast([16, 8, T // 4])
        )
        w1_raw = sbuf("w1_raw", PACK * H, F32, tag="w_raw")
        nc.sync.dma_start(w1_raw[:], w1.rearrange("(p j) c -> p (j c)", j=PACK))
        n1_t = load_list("n1_t", n1)
        n2_t = load_list("n2_t", n2)
        word_table = sbuf("word_table", T, I32)
        nc.sync.dma_start(word_table[:], x_words[0].rearrange("p c r -> p (c r)").bitcast(I32))
        n3_t = load_list("n3_t", n3)
        n4_t = load_list("n4_t", n4)
        n5_t = load_list("n5_t", n5)

        tau_t = sbuf("tau_t", ROW_TILES, F32)
        with nc.allow_non_contiguous_dma(reason="one rate to a partition and tile"):
            nc.sync.dma_start(tau_t[:], tau.rearrange("(u p) o -> p (u o)", p=P))
        gn_t = sbuf("gn_t", PACK, F32)
        nc.gpsimd.dma_start(gn_t[:], gn.rearrange("(p t) o -> p (t o)", t=PACK))
        neg_tau = sbuf("neg_tau", ROW_TILES, F32)
        nc.gpsimd.tensor_scalar(neg_tau[:], tau_t[:], -1.0, 0.0, ALU.mult, ALU.add)
        neg_gn = sbuf("neg_gn", PACK, F32)
        nc.gpsimd.tensor_scalar(neg_gn[:], gn_t[:], -1.0, 0.0, ALU.mult, ALU.add)

        picked_scales = sbuf("picked_scales", S, U8)
        nc.vector.tensor_copy(picked_scales[:], scale_table[:].indirect(offs_t[:]))
        x_plane = sbuf("x_plane", S, U8)
        nc.vector.tensor_copy(x_plane[:].bitcast(I32), picked_scales[:].bitcast(I32))
        for r in range(1, 4):
            nc.sync.dma_start(x_plane[r:P:32, :].bitcast(I32), picked_scales[8 * r : P : 32, :].bitcast(I32))

        w1_bf = sbuf("w1_bf", PACK * H, BF16)
        w1_dst = w1_bf[:].rearrange("p (t m j) -> p m j t", t=PACK, j=PACK)
        w1_src = w1_raw[:].rearrange("p (j m t) -> p m j t", t=PACK, j=PACK)
        nc.scalar.activation(w1_dst[:, :SCALAR_W1], w1_src[:, :SCALAR_W1], ACT.Copy)
        nc.vector.tensor_copy(w1_dst[:, SCALAR_W1:], w1_src[:, SCALAR_W1:])
        w1_codes = sbuf("w1_codes", H, U32)
        w1_plane = sbuf("w1_plane", H, U8)
        for t in range(PACK):
            cols = slice(t * P, (t + 1) * P)
            nc.vector.quantize_mx(
                w1_codes[:, cols].bitcast(FP8X4), w1_plane[:, cols], w1_bf[:, PACK * t * P : PACK * (t + 1) * P]
            )

        w2_raw = sbuf("w2_raw", PACK * N, F32, tag="w_raw")
        nc.sync.dma_start(w2_raw[:], w2.rearrange("(p t) c -> p (t c)", t=PACK))

        y_bank = [[bank("y%d%d" % (c, q), 2 * c + q) for q in range(2)] for c in range(2)]
        y_rows = [sbuf("y_rows%d" % t, S, F32) for t in range(PACK)]
        picked_words = [sbuf("picked_words%d" % c, HALF, U32) for c in range(2)]
        for c in range(2):
            nc.vector.tensor_copy(
                picked_words[c][:], word_table[:].bitcast(U32).indirect(entries(offs_t, c * HALF, HALF))
            )

        def y_psum(c, t, first=0, count=HALF):
            return y_bank[c][t // 2][:, span(t % 2, first, count)]

        def first_product(c, t):
            cols = slice(t * P, (t + 1) * P)
            nc.tensor.matmul_mx(
                y_psum(c, t),
                lhsT=w1_codes[:, cols].bitcast(FP8X4),
                lhsT_scale=w1_plane[:, cols],
                rhs=picked_words[c][:].bitcast(FP8X4),
                rhs_scale=x_plane[:, span(c)],
                start=True,
                stop=True,
            )

        def keep_y(engine, c, t):
            plain_copy(engine, y_rows[t][:, span(c)], y_psum(c, t))

        at1 = [sbuf("at1_%d" % c, PACK * HALF, F32) for c in range(2)]
        at2 = [sbuf("at2_%d" % c, PACK * HALF, F32) for c in range(2)]
        at3 = [sbuf("at3_%d" % c, PACK * HALF, F32) for c in range(2)]
        z_woven = [sbuf("z_woven%d" % c, PACK * HALF, BF16) for c in range(2)]
        z_rows = [sbuf("z_rows%d" % c, PACK * HALF, BF16) for c in range(2)]
        z_codes = [sbuf("z_codes%d" % c, HALF, U32) for c in range(2)]
        z_plane = [sbuf("z_plane%d" % c, HALF, U8) for c in range(2)]

        def fetch_y(engine, c, t, first=0, count=HALF):
            for dst, list_tile in ((at1, n1_t), (at2, n2_t), (at3, n3_t)):
                offsets = entries(list_tile, c * HALF + first, count)
                gather(engine, dst[c][:, span(t, first, count)], y_rows[t], offsets)

        def larger_of_own(c, t, first=0, count=HALF):
            cols = span(t, first, count)
            nc.vector.tensor_tensor(at1[c][:, cols], y_psum(c, t, first, count), at1[c][:, cols], ALU.max)

        def larger_of_others(c, t, first=0, count=HALF):
            cols = span(t, first, count)
            nc.vector.tensor_tensor(at2[c][:, cols], at2[c][:, cols], at3[c][:, cols], ALU.max)

        def gain(c, t, first=0, count=HALF):
            cols = span(t, first, count)
            nc.vector.tensor_scalar(at1[c][:, cols], at1[c][:, cols], gn_t[:, t : t + 1], None, ALU.mult)

        def difference(c, t, first=0, count=HALF):
            cols = span(t, first, count)
            nc.vector.scalar_tensor_tensor(
                z_rows[c][:, cols], at2[c][:, cols], neg_gn[:, t : t + 1], at1[c][:, cols], ALU.mult, ALU.add
            )

        def weave_z(c, first=0, count=HALF):
            cols = slice(first, first + count)
            nc.vector.tensor_copy(
                z_woven[c][:].rearrange("p (j t) -> p j t", t=PACK)[:, cols],
                z_rows[c][:].rearrange("p (t j) -> p j t", t=PACK)[:, cols],
            )

        def quantise_z(c, first=0, count=HALF):
            cols = slice(first, first + count)
            nc.vector.quantize_mx(
                z_codes[c][:, cols].bitcast(FP8X4),
                z_plane[c][:, cols],
                z_woven[c][:, PACK * first : PACK * (first + count)],
            )

        w2_codes = sbuf("w2_codes", N, U32)
        w2_plane = sbuf("w2_plane", N, U8)
        w2_bf = sbuf("w2_bf", PACK * N, BF16)
        w2_dst = w2_bf[:].rearrange("p (m t) -> p m t", t=PACK)
        w2_src = w2_raw[:].rearrange("p (t m) -> p m t", t=PACK)
        for first in (0, N // 2):
            cols = slice(first, first + N // 2)
            nc.gpsimd.tensor_scalar(w2_dst[:, cols], w2_src[:, cols], 1.0, 0.0, ALU.mult, ALU.add)

        h_bank = [bank("h%d" % u, 4 + u) for u in range(ROW_TILES)]
        h_last = {}

        def h_psum(u, first, count):
            if first < LAST:
                return h_bank[u][:, first : first + count]
            return h_last[u][:, :count]

        def second_product(c, first=0, count=HALF):
            for u in range(ROW_TILES):
                if c * HALF + first == LAST:
                    h_last[u] = bank("h_last%d" % u, u)
                cols = slice(u * P, (u + 1) * P)
                nc.tensor.matmul_mx(
                    h_psum(u, c * HALF + first, count),
                    lhsT=w2_codes[:, cols].bitcast(FP8X4),
                    lhsT_scale=w2_plane[:, cols],
                    rhs=z_codes[c][:, first : first + count].bitcast(FP8X4),
                    rhs_scale=z_plane[c][:, first : first + count],
                    start=True,
                    stop=True,
                )

        h_rows = [sbuf("h_rows%d" % u, S, F32) for u in range(ROW_TILES)]
        sz_rows = [sbuf("sz_rows%d" % u, S, F32) for u in range(ROW_TILES)]

        def keep_sz(u, first, count):
            nc.scalar.activation(sz_rows[u][:, first : first + count], h_psum(u, first, count), ACT.Abs)

        def keep_h(engine, u, first, count):
            plain_copy(engine, h_rows[u][:, first : first + count], h_psum(u, first, count))

        for c in range(2):
            first_product(c, 0)
            first_product(c, 2)
            keep_y("scalar", c, 0)
            keep_y("vector", c, 2)
        for c in range(2):
            first_product(c, 1)
            first_product(c, 3)
        fetch_y("scalar", 0, 0)
        fetch_y("vector", 0, 2)
        for c in range(2):
            keep_y("scalar", c, 1)
            keep_y("vector", c, 3)
        fetch_y("scalar", 0, 1)
        fetch_y("vector", 0, 3)
        for t in (2, 0):
            larger_of_own(0, t, 0, 2 * HALF)
        nc.vector.quantize_mx(w2_codes[:].bitcast(FP8X4), w2_plane[:], w2_bf[:])
        for t in (2, 3, 0, 1):
            gain(0, t)
        for t in (2, 0):
            larger_of_others(0, t, 0, 2 * HALF)
        for t in range(PACK):
            difference(0, t)

        pieces = [(t, 0, HALF) for t in range(PACK - 1)] + [(PACK - 1, 0, QUARTER), (PACK - 1, QUARTER, QUARTER)]
        for piece in pieces:
            fetch_y("scalar", 1, *piece)
        larger_of_own(1, *pieces[0])
        weave_z(0)
        larger_of_others(1, *pieces[0])
        quantise_z(0)
        second_product(0)
        gain(1, *pieces[0])
        for done, piece in zip(pieces[:3], pieces[1:4]):
            larger_of_own(1, *piece)
            difference(1, *done)
            gain(1, *piece)
            larger_of_others(1, *piece)
        larger_of_own(1, *pieces[4])
        difference(1, *pieces[3])
        gain(1, *pieces[4])
        weave_z(1, 0, QUARTER)
        larger_of_others(1, *pieces[4])
        quantise_z(1, 0, QUARTER)
        difference(1, *pieces[4])
        weave_z(1, QUARTER, QUARTER)

        for u in range(ROW_TILES):
            keep_sz(u, 0, HALF)
            keep_h("scalar", u, 0, HALF)
        second_product(1, 0, QUARTER)
        quantise_z(1, QUARTER, QUARTER)
        for u in range(ROW_TILES):
            keep_sz(u, HALF, QUARTER)
            keep_h("scalar", u, HALF, QUARTER)
        second_product(1, QUARTER, QUARTER)

        ea = [sbuf("ea%d" % u, S, F32) for u in range(ROW_TILES)]
        res = [sbuf("res%d" % u, S, F32) for u in range(ROW_TILES)]

        def fetch_ea(u, first, count=HALF):
            nc.scalar.activation(
                ea[u][:, first : first + count],
                sz_rows[u][:].indirect(entries(n4_t, first, count)),
                ACT.Exp,
                scale=neg_tau[:, u : u + 1],
            )

        def fetch_h(engine, u, c):
            gather(engine, res[u][:, span(c)], h_rows[u], entries(n5_t, c * HALF, HALF))

        def less_fetched(u):
            for first, count in H_PIECES:
                cols = slice(first, first + count)
                nc.vector.tensor_tensor(res[u][:, cols], h_psum(u, first, count), res[u][:, cols], ALU.subtract)

        def finish(engine, queue, u, first, count=HALF):
            cols = slice(first, first + count)
            engine.tensor_tensor(res[u][:, cols], res[u][:, cols], ea[u][:, cols], ALU.mult)
            queue.dma_start(out[u * P : (u + 1) * P, cols], res[u][:, cols])

        keep_h("vector", 0, LAST, QUARTER)
        keep_sz(1, LAST, QUARTER)
        keep_sz(0, LAST, QUARTER)
        keep_h("vector", 1, LAST, QUARTER)
        final = ROW_TILES - 1
        for u in range(final):
            for c in range(2):
                fetch_h("vector", u, c)
            for c in range(2):
                fetch_ea(u, c * HALF)
            if u + 2 < ROW_TILES:
                keep_h("vector", u + 2, LAST, QUARTER)
                keep_sz(u + 2, LAST, QUARTER)
            if u > 0:
                fetch_h("scalar", final, u - 1)
            less_fetched(u)
            finish(nc.gpsimd, nc.sync, u, 0)
            if u < final - 1:
                finish(nc.gpsimd, nc.sync, u, HALF)
        for first, count in H_PIECES:
            fetch_ea(final, first, count)
        less_fetched(final)
        finish(nc.vector, nc.scalar, final - 1, HALF)
        for first, count in H_PIECES:
            finish(nc.vector, nc.scalar, final, first, count)
